import numpy as np
import ml_dtypes


def mxq(x, axis, fmt="e4m3"):
    dtype, down = {"e4m3": (ml_dtypes.float8_e4m3fn, 7), "e5m2": (ml_dtypes.float8_e5m2, 14)}[fmt]
    v = np.moveaxis(np.asarray(x, np.float32).astype(ml_dtypes.bfloat16).astype(np.float64), axis, -1)
    blocks = v.reshape(v.shape[:-1] + (-1, 32))
    amax = np.abs(blocks).max(-1, keepdims=True)
    byte = np.maximum(np.where(amax > 0, np.frexp(amax)[1] - 1 + 127, 0) - down, 1)
    scale = np.exp2(byte - 127.0)
    codes = (blocks / scale).astype(np.float32).astype(dtype).astype(np.float64)
    return np.moveaxis((codes * scale).reshape(v.shape), -1, axis)


WIDE = False


def mx_kscale(k):
    if not WIDE:
        return np.ones(k)
    levels = np.array([10, -10, 5, -5, 0])
    if k % 512:
        return np.exp2(np.random.permutation(np.resize(levels, k // 32))).repeat(32)
    a = np.empty((k // 512, 16))
    for p in range(k // 512):
        a[p, :8] = np.random.permutation(np.resize(levels, 8))
        for g in range(8):
            far = levels[np.abs(levels - a[p, g]) >= 10]
            a[p, g + 8] = far[np.random.randint(len(far))]
    return np.exp2(a.ravel()).repeat(32)


BF16 = ml_dtypes.bfloat16


def bf(x):
    return np.asarray(x, np.float32).astype(BF16)


def f64(x):
    return np.asarray(x).astype(np.float64)


E2M1 = np.array([0.0, 0.5, 1.0, 1.5, 2.0, 3.0, 4.0, 6.0, -0.0, -0.5, -1.0, -1.5, -2.0, -3.0, -4.0, -6.0])


def pack_weight(w, fmt):
    k, n = w.shape
    w = f64(bf(w)).reshape(k // 32, 32, n)
    amax = np.abs(w).max(1)
    if fmt == "e4m3":
        byte = np.frexp(amax)[1] - 1 + 127 - 7
    else:
        mant, ex = np.frexp(amax / 6.0)
        byte = np.where(mant > 0.5, ex, ex - 1) + 127
    byte = np.clip(np.where(amax > 0, byte, 1), 1, 254)
    scaled = (w * np.exp2(127.0 - byte)[:, None, :]).reshape(k, n).astype(np.float32)
    by_word = np.ascontiguousarray(scaled.reshape(k // 512, 128, 4, n).transpose(0, 1, 3, 2))
    if fmt == "e4m3":
        words = by_word.astype(ml_dtypes.float8_e4m3fn).view(np.uint8)
    else:
        c = by_word.astype(ml_dtypes.float4_e2m1fn).view(np.uint8) & 0xF
        words = c[..., 0::2] | (c[..., 1::2] << 4)
    return np.ascontiguousarray(words), np.ascontiguousarray(byte.astype(np.uint8).reshape(k // 512, 16, n))


def unpack_weight(words, scales, fmt):
    g, p, n, _ = words.shape
    if fmt == "e4m3":
        vals = np.ascontiguousarray(words).view(ml_dtypes.float8_e4m3fn).astype(np.float64)
    else:
        nib = np.empty((g, p, n, 4), np.uint8)
        nib[..., 0::2] = words & 0xF
        nib[..., 1::2] = words >> 4
        vals = E2M1[nib]
    vals = vals * np.repeat(np.exp2(scales.astype(np.float64) - 127.0), 8, axis=1)[..., None]
    return vals.transpose(0, 1, 3, 2).reshape(g * 512, n)
def pack4(w):
    words, scales = pack_weight(w, "e2m1")
    return words.reshape(words.shape[0], 128, -1), scales


def unpack4(words, scales):
    return unpack_weight(words.reshape(words.shape[0], 128, -1, 2), scales, "e2m1")


E4M3FN = np.array([(-1.0 if i & 128 else 1.0) * ((1.0 + (i & 7) / 8.0) * 2.0 ** (((i >> 3) & 15) - 7) if i & 120 else (i & 7) * 2.0 ** -9) for i in range(256)])


def e4m3fn_bytes(y):
    return np.clip(np.asarray(y, np.float64), -448.0, 448.0).astype(np.float32).astype(ml_dtypes.float8_e4m3fn).view(np.uint8)


def e4m3fn_values(b):
    return E4M3FN[b]


T, D, N = 1024, 1024, 1024

ETA = 0.8
GAMMA_KEEP = 0.85
GAMMA_MIX = 0.15


def draw0():
    s, t = mx_kscale(D), mx_kscale(D)[::-1]
    v = bf(np.random.standard_normal((T, D)) * s)
    pinv_words, pinv_scales = pack4(np.random.standard_normal((D, D)) / np.sqrt(D) / s[:, None])
    surp = bf(np.random.standard_normal(T))
    m = bf(np.random.standard_normal((T, D)) * 0.7)
    g = bf((1.0 + 0.1 * np.random.standard_normal(D)) * t)
    arms_words, arms_scales = pack4((np.random.standard_normal((N, D)) / np.sqrt(D) / t).T)
    return {
        "v": v,
        "pinv_words": pinv_words,
        "pinv_scales": pinv_scales,
        "surp": surp,
        "m": m,
        "g": g,
        "arms_words": arms_words,
        "arms_scales": arms_scales,
        "logw": bf(np.random.standard_normal((T, N)) * 0.5),
        "mu": bf(np.random.uniform(0.5, 2.5, N)),
    }


def estimate_loss(v, pinv, surp, m):
    z = mxq(v, 1, "e4m3") @ pinv
    return m + surp[:, None] * z


def over_mean(x):
    return x / np.mean(x, axis=-1, keepdims=True)


def core(v, pinv_words, pinv_scales, surp, m, g, arms_words, arms_scales, logw, mu):
    lhat = estimate_loss(f64(v), unpack4(pinv_words, pinv_scales), f64(surp), f64(m))
    u = lhat * f64(g)[None, :]
    s = mxq(u, 1, "e4m3") @ unpack4(arms_words, arms_scales)
    y = f64(logw) - ETA * s
    r = over_mean(np.exp(y))
    mu = f64(mu)
    q = GAMMA_KEEP * r + (GAMMA_MIX * mu / np.mean(mu))[None, :]
    return np.log(q)


def setup_inputs():
    drawn = draw0()
    full = np.asarray(drawn['v']).astype(np.float64)
    scale = (np.abs(full).reshape(1024, 8, 128).max(axis=(2,)) / 448.0).astype(np.float32)
    given = {}
    for key, value in drawn.items():
        if key == 'v':
            given['v_bytes'] = e4m3fn_bytes(full / np.repeat(scale.astype(np.float64), 128, axis=1))
            given['v_scale'] = scale
        else:
            given[key] = value
    return given


def reference(v_bytes, v_scale, pinv_words, pinv_scales, surp, m, g, arms_words, arms_scales, logw, mu):
    return core(e4m3fn_values(v_bytes) * np.repeat(v_scale.astype(np.float64), 128, axis=1), pinv_words, pinv_scales, surp, m, g, arms_words, arms_scales, logw, mu)

@@ -1,0 +1,313 @@
+from contextlib import ExitStack
+
+import concourse.mybir as mybir
+from concourse.masks import make_identity
+
+T, D, N = 1024, 1024, 1024
+P = 128
+NT = T // P
+FLOPS = 2 * T * D * D + 2 * T * D * N
+
+F32 = mybir.dt.float32
+BF16 = mybir.dt.bfloat16
+I32 = mybir.dt.int32
+U32 = mybir.dt.uint32
+U8 = mybir.dt.uint8
+FP8 = mybir.dt.float8_e4m3fn
+E4M3X4 = mybir.dt.float8_e4m3fn_x4
+E2M1X4 = mybir.dt.float4_e2m1fn_x4
+ALU = mybir.AluOpType
+ACT = mybir.ActivationFunctionType
+
+ETA = 0.8
+KEEP = 0.85
+MIX = 0.15
+
+WV = [5,5,5,3,0,0,0,0]
+LP = [3,4,5]
+ORDER = "WS:0 WV:0 WS:1 WV:1 Tv:0 WS:2 WV:2 Tv:1 E:0 WV:3 E:1 Tv:2 Qv:0 WS:3 Mz:0.1 Qv:1 Mz:0.0 E:2 prep:0 L:0.1 WS:4 Tv:3 Qv:2 L:0.0 Tu:0.1 Mz:1.1 G:0.1 E:3 Mz:1.0 L:1.1 WS:6 Tu:0.0 L:1.0 Tu:1.1 G:0.0 Tv:4 WS:7 G:1.1 Mz:2.0 Qu:0 Tu:1.0 E:4 L:2.0 Ms:0.0 WS:5 G:1.0 Ms:0.1 Y:0.0 Tu:2.0 Qu:1 Mz:2.1 Y:0.1 G:2.0 Ms:1.1 X:0 L:2.1 Ms:1.0 Y:1.1 Tu:2.1 Y:1.0 Tv:6 Tv:5 Qv:3 X:1 G:2.1 Mz:3.0 Qv:4 Mz:3.1 Qu:2 E:5 mu:0 Ms:2.1 L:3.0 Qv:5 Ms:2.0 L:3.1 Y:2.1 Tu:3.0 E:6 Y:2.0 Qv:6 Tu:3.1 X:2 G:3.0 Mz:4.1 G:3.1 Mz:4.0 c:0.3 L:4.1 Qu:3 R:0 Ms:3.1 L:4.0 Tu:4.1 R:1 Tu:4.0 G:4.1 Ms:3.0 G:4.0 Mz:5.1 Y:3.0 Mz:5.0 L:5.1 Qu:4 Tv:7 L:5.0 Y:3.1 Ms:4.0 R:2 E:7 X:3 Mz:6.0 Y:4.0 Ms:4.1 Qv:7 Tu:5.0 N:0 N:1 N:2 Y:4.1 Tu:5.1 L:6.0 G:5.0 Mz:6.1 G:5.1 Mz:7.0 L:6.1 Tu:6.0 Qu:5 Mz:7.1 L:7.0 Ms:5.1 G:6.0 Ms:5.0 L:7.1 Tu:6.1 Y:5.1 Tu:7.0 G:6.1 G:7.0 Tu:7.1 X:4 Qu:6 Y:5.0 Ms:6.1 G:7.1 X:5 Ms:6.0 Y:6.1 Qu:7 Y:6.0 Ms:7.1 Ms:7.0 X:6 Y:7.1 Y:7.0 c:3.7 X:7 R:3 R:5 R:4 N:3 R:6 N:4 c:7.8 R:7 N:6 N:7 N:5".split(" ")
+
+
+def tile_controlvariateexp2linearbanditpolicy_d1p_kernel(
+    tc, v_bytes, v_scale, pinv_words, pinv_scales, surp, m, g, arms_words, arms_scales, logw, mu, out
+):
+    nc = tc.nc
+    with ExitStack() as ctx:
+        keep = ctx.enter_context(tc.tile_pool(name="keep", bufs=1))
+        psum = ctx.enter_context(tc.psum_pool(name="psum", bufs=1))
+        ctx.enter_context(tc.manual_schedule())
+
+        def load_scales(hbm, name, eng):
+            t = keep.tile([P, 2, N], U8, name=name, align_bytes=64)
+            nc.gpsimd.memset(t[:].bitcast(I32), 0)
+            view = hbm.bitcast(I32)
+            for q in range(4):
+                eng.dma_start(
+                    out=t[:].bitcast(I32)[32 * q : 32 * q + 4, :, :],
+                    in_=view[:, 4 * q : 4 * q + 4, :].rearrange("g q n -> q g n"),
+                )
+            return t
+
+        def load_words(hbm, name):
+            t = keep.tile([P, 2, 2 * N], U8, name=name, align_bytes=64)
+            nc.sync.dma_start(out=t[:].bitcast(I32), in_=hbm.bitcast(I32).rearrange("g p c -> p g c"))
+            return t
+
+        vs = keep.tile([P, NT, 8], F32, name="vscale")
+        nc.sync.dma_start(out=vs[:], in_=v_scale.rearrange("(p i) j -> p i j", i=NT))
+        v_rows = v_bytes.rearrange("(p i) k -> p i k", i=NT)
+        m_rows = m.rearrange("(p i) d -> p i d", i=NT)
+        lw_rows = logw.rearrange("(p i) n -> p i n", i=NT)
+        out_rows = out.rearrange("(p i) n -> p i n", i=NT)
+
+        v_u8 = {}
+
+        def load_v(a, b):
+            t = keep.tile([P, b - a, D], U8, name="v_u8_%d" % a, align_bytes=64)
+            nc.sync.dma_start(out=t[:], in_=v_rows[:, a:b, :])
+            for i in range(a, b):
+                v_u8[i] = t[:, i - a, :]
+
+        m_sb = {}
+        lw_sb = {}
+
+        def load_rows(rows, into, a, b, name):
+            t = keep.tile([P, b - a, 1024], BF16, name="%s_%d" % (name, a), align_bytes=64)
+            nc.sync.dma_start(out=t[:], in_=rows[:, a:b, :])
+            for i in range(a, b):
+                into[i] = t[:, i - a, :]
+
+        load_v(0, 1)
+        load_v(1, 2)
+        ps = load_scales(pinv_scales, "ps", nc.scalar)
+        pw = load_words(pinv_words, "pw")
+        load_v(2, 4)
+        load_rows(m_rows, m_sb, 0, 2, "m")
+        load_v(4, 8)
+        load_rows(m_rows, m_sb, 2, 4, "m")
+        aw = load_words(arms_words, "aw")
+        load_rows(lw_rows, lw_sb, 0, 2, "lw")
+        load_rows(m_rows, m_sb, 4, 8, "m")
+        load_rows(lw_rows, lw_sb, 2, 4, "lw")
+        load_rows(lw_rows, lw_sb, 4, 8, "lw")
+        mu_bc = keep.tile([P, N], BF16, name="mu_bc")
+        nc.sync.dma_start(out=mu_bc[:], in_=mu.partition_broadcast(P))
+
+        ident = keep.tile([P, P], F32, name="ident")
+        make_identity(nc, ident[:])
+        sp16 = keep.tile([P, NT], BF16, name="sp16")
+        nc.gpsimd.dma_start(out=sp16[:], in_=surp.rearrange("(p i) -> p i", i=NT))
+        g16 = keep.tile([P, 2, 4], BF16, name="g16")
+        nc.gpsimd.dma_start(out=g16[:], in_=g.rearrange("(h p t) -> p h t", h=2, t=4))
+        asc = load_scales(arms_scales, "asc", nc.gpsimd)
+        mu_col = keep.tile([P, 8], BF16, name="mu_col")
+        nc.gpsimd.dma_start(out=mu_col[:], in_=mu.rearrange("(p i) -> p i", i=8))
+        ones = keep.tile([P, P], F32, name="ones")
+        nc.gpsimd.memset(ones[:], 1.0)
+
+        sums = keep.tile([P, NT], F32, name="sums")
+        rec = keep.tile([P, NT], F32, name="rec")
+        cc = keep.tile([P, NT], F32, name="cc")
+        sp = keep.tile([P, NT], F32, name="sp")
+        ident16 = keep.tile([P, P], BF16, name="ident16")
+        mu_part = keep.tile([P, 1], F32, name="mu_part")
+        mu_sum = keep.tile([P, 1], F32, name="mu_sum")
+        mu_rec = keep.tile([P, 1], F32, name="mu_rec")
+        kappa = keep.tile([P, 1], F32, name="kappa")
+
+        def prep():
+            nc.vector.tensor_copy(out=sp[:], in_=sp16[:])
+            nc.vector.tensor_copy(out=ident16[:], in_=ident[:])
+
+        def prep_mu():
+            nc.vector.tensor_reduce(out=mu_part[:], in_=mu_col[:], axis=mybir.AxisListType.X, op=ALU.add)
+            mu_tot = psum.tile([P, 1], F32, name="ut0")
+            nc.tensor.matmul(mu_tot[:], lhsT=ones[:], rhs=mu_part[:], start=True, stop=True)
+            nc.vector.tensor_copy(out=mu_sum[:], in_=mu_tot[:])
+            nc.vector.reciprocal(out=mu_rec[:], in_=mu_sum[:])
+            nc.vector.tensor_scalar(out=kappa[:], in0=mu_rec[:], scalar1=MIX * N, scalar2=None, op0=ALU.mult)
+
+        vbf = {}
+        vq = {}
+        vq_s = {}
+        v4 = {}
+        lh = {}
+        u4 = {}
+        uq = {}
+        uq_s = {}
+        e_t = {}
+
+        def widen(i, on_v):
+            if i not in vbf:
+                vbf[i] = keep.tile([P, D], BF16, name="vbf", bufs=8, align_bytes=64)
+            nv = WV[i]
+            for j in range(0 if on_v else nv, nv if on_v else 8):
+                src = v_u8[i][:, P * j : P * (j + 1)].bitcast(FP8)
+                dst = vbf[i][:, P * j : P * (j + 1)]
+                col = vs[:, i, j : j + 1]
+                if j < nv:
+                    nc.vector.tensor_scalar(out=dst, in0=src, scalar1=col, scalar2=None, op0=ALU.mult)
+                else:
+                    nc.scalar.activation(out=dst, in_=src, func=ACT.Copy, scale=col)
+
+        tv = {}
+
+        def turn_v(i):
+            tv[i] = psum.tile([P, 2, 2, P], F32, name="tv", bufs=2)
+            words = vbf[i][:].bitcast(F32)
+            for gg in range(2):
+                for u in range(2):
+                    nc.tensor.transpose(tv[i][:, gg, u, :], words[:, 256 * gg + u : 256 * (gg + 1) : 2], ident[:])
+
+        def take_v(i):
+            v4[i] = keep.tile([P, 2, P, 4], BF16, name="v4", bufs=8, align_bytes=64)
+            nc.scalar.copy(
+                out=v4[i][:].rearrange("p g r t -> p (g r t)").bitcast(F32).rearrange("p (g r u) -> p g r u", g=2, u=2),
+                in_=tv[i][:].rearrange("p g u r -> p g r u"),
+            )
+
+        def quant(src, i, codes, scales, name, nb):
+            codes[i] = keep.tile([P, 2, P], U32, name=name + "_codes", bufs=nb, align_bytes=64)
+            scales[i] = keep.tile([P, 2, P], U8, name=name + "_sc", bufs=nb, align_bytes=64)
+            nc.vector.quantize_mx(
+                out=codes[i][:].rearrange("p g r -> p (g r)").bitcast(E4M3X4),
+                scales=scales[i][:].rearrange("p g r -> p (g r)"),
+                in_=src[i][:].rearrange("p g r t -> p (g r t)"),
+            )
+
+        def mm(i, h, codes, scales, words, wscales, name, into):
+            bank = psum.tile([P, 512], F32, name="%s%d" % (name, h))
+            for gg in range(2):
+                nc.tensor.matmul_mx(
+                    out=bank[:],
+                    lhsT=codes[i][:, gg, :].bitcast(E4M3X4),
+                    lhsT_scale=scales[i][:, gg, :],
+                    rhs=words[:, gg, 1024 * h : 1024 * (h + 1)].bitcast(E2M1X4),
+                    rhs_scale=wscales[:, gg, 512 * h : 512 * (h + 1)],
+                    start=(gg == 0),
+                    stop=(gg == 1),
+                )
+            into[i, h] = bank
+
+        z = {}
+        s = {}
+
+        def lhat(i, h):
+            lh[i, h] = keep.tile([P, 4, P], F32, name="lh%d" % h, bufs=4, align_bytes=64)
+            zv = z[i, h][:].rearrange("q (p t) -> q t p", t=4)
+            if i in LP:
+                nc.scalar.activation(out=lh[i, h][:], in_=zv, func=ACT.Copy, scale=sp[:, i : i + 1])
+                return
+            nc.vector.scalar_tensor_tensor(
+                out=lh[i, h][:],
+                in0=zv,
+                scalar=sp[:, i : i + 1],
+                in1=m_sb[i][:, 512 * h : 512 * (h + 1)].rearrange("q (p t) -> q t p", t=4),
+                op0=ALU.mult,
+                op1=ALU.add,
+            )
+
+        ut = {}
+
+        def turn_u(i, h):
+            bank = psum.tile([P, 4, P], F32, name="ut%d" % h)
+            for t in range(4):
+                if i in LP:
+                    nc.tensor.matmul(
+                        bank[:, t, :], lhsT=m_sb[i][:, 512 * h + t : 512 * (h + 1) : 4], rhs=ident16[:], start=True, stop=False
+                    )
+                    nc.tensor.matmul(bank[:, t, :], lhsT=lh[i, h][:, t, :], rhs=ident[:], is_transpose=True, start=False, stop=True)
+                else:
+                    nc.tensor.transpose(bank[:, t, :], lh[i, h][:, t, :], ident[:])
+            ut[i, h] = bank
+
+        def gain(i, h):
+            if i not in u4:
+                u4[i] = keep.tile([P, 2, P, 4], BF16, name="u4", bufs=3, align_bytes=64)
+            nc.vector.tensor_tensor(
+                out=u4[i][:, h],
+                in0=ut[i, h][:].rearrange("p t r -> p r t"),
+                in1=g16[:, h, :].unsqueeze(1).to_broadcast([P, P, 4]),
+                op=ALU.mult,
+            )
+
+        y = {}
+
+        def negy(i, h):
+            if i not in y:
+                y[i] = keep.tile([P, N], F32, name="y", bufs=4)
+            nc.vector.scalar_tensor_tensor(
+                out=y[i][:, 512 * h : 512 * (h + 1)],
+                in0=s[i, h][:],
+                scalar=ETA,
+                in1=lw_sb[i][:, 512 * h : 512 * (h + 1)],
+                op0=ALU.mult,
+                op1=ALU.subtract,
+            )
+
+        def expo(i):
+            e_t[i] = keep.tile([P, N], F32, name="e_%d" % i)
+            nc.scalar.activation(
+                out=e_t[i][:], in_=y[i][:], func=ACT.Exp, scale=-1.0, bias=y[i][:, 0:1], accum_out=sums[:, i : i + 1]
+            )
+
+        def row_factor(a, b):
+            nc.vector.reciprocal(out=rec[:, a:b], in_=sums[:, a:b])
+            nc.vector.tensor_scalar(
+                out=cc[:, a:b], in0=rec[:, a:b], scalar1=mu_sum[:, 0:1], scalar2=KEEP / MIX, op0=ALU.mult, op1=ALU.mult
+            )
+
+        def mix(i):
+            nc.vector.scalar_tensor_tensor(
+                out=e_t[i][:], in0=e_t[i][:], scalar=cc[:, i : i + 1], in1=mu_bc[:], op0=ALU.mult, op1=ALU.add
+            )
+
+        def log_store(i):
+            o = keep.tile([P, N], F32, name="o", bufs=4)
+            nc.scalar.activation(out=o[:], in_=e_t[i][:], func=ACT.Ln, scale=kappa[:, 0:1])
+            nc.sync.dma_start(out=out_rows[:, i, :], in_=o[:])
+
+        def run(op):
+            k, a = op.split(":")
+            a = [int(x) for x in a.split(".")]
+            i = a[0]
+            h = a[-1]
+            if k == "WV":
+                widen(i, True)
+            elif k == "WS":
+                widen(i, False)
+            elif k == "Tv":
+                turn_v(i)
+            elif k == "E":
+                take_v(i)
+            elif k == "Qv":
+                quant(v4, i, vq, vq_s, "v", 8)
+            elif k == "Mz":
+                mm(i, h, vq, vq_s, pw, ps, "z", z)
+            elif k == "L":
+                lhat(i, h)
+            elif k == "Tu":
+                turn_u(i, h)
+            elif k == "G":
+                gain(i, h)
+            elif k == "Qu":
+                quant(u4, i, uq, uq_s, "u", 3)
+            elif k == "Ms":
+                mm(i, h, uq, uq_s, aw, asc, "s", s)
+            elif k == "Y":
+                negy(i, h)
+            elif k == "X":
+                expo(i)
+            elif k == "prep":
+                prep()
+            elif k == "mu":
+                prep_mu()
+            elif k == "c":
+                row_factor(i, h)
+            elif k == "R":
+                mix(i)
+            elif k == "N":
+                log_store(i)
+
+        for op in ORDER:
+            run(op)

@@ -24,8 +24,9 @@ KEEP = 0.85
 MIX = 0.15
 
 WV = [5,5,5,3,0,0,0,0]
-LP = [3,4,5]
-ORDER = "WS:0 WV:0 WS:1 WV:1 Tv:0 WS:2 WV:2 Tv:1 E:0 WV:3 E:1 Tv:2 Qv:0 WS:3 Mz:0.1 Qv:1 Mz:0.0 E:2 prep:0 L:0.1 WS:4 Tv:3 Qv:2 L:0.0 Tu:0.1 Mz:1.1 G:0.1 E:3 Mz:1.0 L:1.1 WS:6 Tu:0.0 L:1.0 Tu:1.1 G:0.0 Tv:4 WS:7 G:1.1 Mz:2.0 Qu:0 Tu:1.0 E:4 L:2.0 Ms:0.0 WS:5 G:1.0 Ms:0.1 Y:0.0 Tu:2.0 Qu:1 Mz:2.1 Y:0.1 G:2.0 Ms:1.1 X:0 L:2.1 Ms:1.0 Y:1.1 Tu:2.1 Y:1.0 Tv:6 Tv:5 Qv:3 X:1 G:2.1 Mz:3.0 Qv:4 Mz:3.1 Qu:2 E:5 mu:0 Ms:2.1 L:3.0 Qv:5 Ms:2.0 L:3.1 Y:2.1 Tu:3.0 E:6 Y:2.0 Qv:6 Tu:3.1 X:2 G:3.0 Mz:4.1 G:3.1 Mz:4.0 c:0.3 L:4.1 Qu:3 R:0 Ms:3.1 L:4.0 Tu:4.1 R:1 Tu:4.0 G:4.1 Ms:3.0 G:4.0 Mz:5.1 Y:3.0 Mz:5.0 L:5.1 Qu:4 Tv:7 L:5.0 Y:3.1 Ms:4.0 R:2 E:7 X:3 Mz:6.0 Y:4.0 Ms:4.1 Qv:7 Tu:5.0 N:0 N:1 N:2 Y:4.1 Tu:5.1 L:6.0 G:5.0 Mz:6.1 G:5.1 Mz:7.0 L:6.1 Tu:6.0 Qu:5 Mz:7.1 L:7.0 Ms:5.1 G:6.0 Ms:5.0 L:7.1 Tu:6.1 Y:5.1 Tu:7.0 G:6.1 G:7.0 Tu:7.1 X:4 Qu:6 Y:5.0 Ms:6.1 G:7.1 X:5 Ms:6.0 Y:6.1 Qu:7 Y:6.0 Ms:7.1 Ms:7.0 X:6 Y:7.1 Y:7.0 c:3.7 X:7 R:3 R:5 R:4 N:3 R:6 N:4 c:7.8 R:7 N:6 N:7 N:5".split(" ")
+LP = [4,5]
+WH = [[(0, 1, 2), (3,)], [(4, 5), (6, 7)]]
+ORDER = "WS:0.0 WV:0.0 Tv:0.0 WS:0.1 WV:0.1 E:0.0 Tv:0.1 E:0.1 WS:1 WV:1 Qv:0.0 Qv:0.1 Tv:1 Mz:0.1 E:1 Mz:0.0 WS:2 WV:2 WS:3 prep:0 L:0.1 Tv:2 L:0.0 Tu:0.1 Qv:1 E:2 Tu:0.0 WV:3 WS:4 G:0.1 Mz:1.1 G:0.0 Mz:1.0 L:1.1 WS:7 Tv:3 L:1.0 Tu:1.1 Qv:2 Tv:4 E:3 Qu:0 G:1.1 Tu:1.0 WS:6 Ms:0.1 Qv:3 G:1.0 Ms:0.0 E:4 Y:0.1 Mz:2.1 WS:5 Y:0.0 Mz:2.0 L:2.1 Tv:6 L:2.0 X:0 Tu:2.1 Qu:1 Tu:2.0 Qv:4 E:6 G:2.1 Ms:1.1 G:2.0 Ms:1.0 Y:1.1 Mz:3.1 Y:1.0 Mz:3.0 Qu:2 Tv:5 X:1 Qv:6 L:3.0 mu:0 Ms:2.0 L:3.1 E:5 Ms:2.1 Y:2.0 Tu:3.1 Y:2.1 Tu:3.0 G:3.1 Mz:4.0 X:2 G:3.0 Tv:7 Qv:5 L:4.0 Qu:3 Mz:4.1 c:0.3 E:7 R:0 Ms:3.0 L:4.1 Ms:3.1 Qv:7 Mz:5.1 Y:3.0 Tu:4.1 Y:3.1 L:5.1 R:2 X:3 Mz:5.0 Tu:4.0 G:4.1 L:5.0 R:1 Tu:5.1 Mz:6.0 G:4.0 N:0 N:1 N:2 G:5.1 Mz:6.1 Qu:4 Tu:5.0 L:6.0 L:6.1 Ms:4.0 G:5.0 Mz:7.1 Y:4.0 Mz:7.0 Qu:5 Ms:4.1 L:7.1 Ms:5.0 L:7.0 Tu:6.0 Y:4.1 Tu:6.1 Y:5.0 Ms:5.1 G:6.0 X:4 G:6.1 Tu:7.0 Y:5.1 Tu:7.1 Qu:6 X:5 G:7.0 Ms:6.0 G:7.1 Ms:6.1 Y:6.0 Qu:7 Y:6.1 Ms:7.0 Ms:7.1 X:6 Y:7.0 Y:7.1 X:7.0 c:3.7 R:3 X:7.1 c:7.8 R:4 R:7 N:3 R:6 N:4 R:5 N:7 N:6 N:5.0".split(" ")
 
 
 def tile_controlvariateexp2linearbanditpolicy_d1p_kernel(
@@ -39,7 +40,7 @@ def tile_controlvariateexp2linearbanditpolicy_d1p_kernel(
 
         def load_scales(hbm, name, eng):
             t = keep.tile([P, 2, N], U8, name=name, align_bytes=64)
-            nc.gpsimd.memset(t[:].bitcast(I32), 0)
+            nc.vector.memset(t[:].bitcast(I32), 0)
             view = hbm.bitcast(I32)
             for q in range(4):
                 eng.dma_start(
@@ -52,6 +53,10 @@ def tile_controlvariateexp2linearbanditpolicy_d1p_kernel(
             t = keep.tile([P, 2, 2 * N], U8, name=name, align_bytes=64)
             nc.sync.dma_start(out=t[:].bitcast(I32), in_=hbm.bitcast(I32).rearrange("g p c -> p g c"))
             return t
+
+        ident = keep.tile([P, P], F32, name="ident")
+        make_identity(nc, ident[:])
+        ident16 = keep.tile([P, P], BF16, name="ident16")
 
         vs = keep.tile([P, NT, 8], F32, name="vscale")
         nc.sync.dma_start(out=vs[:], in_=v_scale.rearrange("(p i) j -> p i j", i=NT))
@@ -79,27 +84,26 @@ def tile_controlvariateexp2linearbanditpolicy_d1p_kernel(
 
         load_v(0, 1)
         load_v(1, 2)
-        ps = load_scales(pinv_scales, "ps", nc.scalar)
+        ps = load_scales(pinv_scales, "ps", nc.sync)
         pw = load_words(pinv_words, "pw")
+        load_rows(m_rows, m_sb, 0, 1, "m")
         load_v(2, 4)
-        load_rows(m_rows, m_sb, 0, 2, "m")
+        load_rows(m_rows, m_sb, 1, 2, "m")
         load_v(4, 8)
-        load_rows(m_rows, m_sb, 2, 4, "m")
+        asc = load_scales(arms_scales, "asc", nc.sync)
         aw = load_words(arms_words, "aw")
         load_rows(lw_rows, lw_sb, 0, 2, "lw")
+        load_rows(m_rows, m_sb, 2, 4, "m")
         load_rows(m_rows, m_sb, 4, 8, "m")
         load_rows(lw_rows, lw_sb, 2, 4, "lw")
         load_rows(lw_rows, lw_sb, 4, 8, "lw")
         mu_bc = keep.tile([P, N], BF16, name="mu_bc")
         nc.sync.dma_start(out=mu_bc[:], in_=mu.partition_broadcast(P))
 
-        ident = keep.tile([P, P], F32, name="ident")
-        make_identity(nc, ident[:])
         sp16 = keep.tile([P, NT], BF16, name="sp16")
         nc.gpsimd.dma_start(out=sp16[:], in_=surp.rearrange("(p i) -> p i", i=NT))
         g16 = keep.tile([P, 2, 4], BF16, name="g16")
         nc.gpsimd.dma_start(out=g16[:], in_=g.rearrange("(h p t) -> p h t", h=2, t=4))
-        asc = load_scales(arms_scales, "asc", nc.gpsimd)
         mu_col = keep.tile([P, 8], BF16, name="mu_col")
         nc.gpsimd.dma_start(out=mu_col[:], in_=mu.rearrange("(p i) -> p i", i=8))
         ones = keep.tile([P, P], F32, name="ones")
@@ -109,7 +113,6 @@ def tile_controlvariateexp2linearbanditpolicy_d1p_kernel(
         rec = keep.tile([P, NT], F32, name="rec")
         cc = keep.tile([P, NT], F32, name="cc")
         sp = keep.tile([P, NT], F32, name="sp")
-        ident16 = keep.tile([P, P], BF16, name="ident16")
         mu_part = keep.tile([P, 1], F32, name="mu_part")
         mu_sum = keep.tile([P, 1], F32, name="mu_sum")
         mu_rec = keep.tile([P, 1], F32, name="mu_rec")
@@ -117,7 +120,6 @@ def tile_controlvariateexp2linearbanditpolicy_d1p_kernel(
 
         def prep():
             nc.vector.tensor_copy(out=sp[:], in_=sp16[:])
-            nc.vector.tensor_copy(out=ident16[:], in_=ident[:])
 
         def prep_mu():
             nc.vector.tensor_reduce(out=mu_part[:], in_=mu_col[:], axis=mybir.AxisListType.X, op=ALU.add)
@@ -127,6 +129,7 @@ def tile_controlvariateexp2linearbanditpolicy_d1p_kernel(
             nc.vector.reciprocal(out=mu_rec[:], in_=mu_sum[:])
             nc.vector.tensor_scalar(out=kappa[:], in0=mu_rec[:], scalar1=MIX * N, scalar2=None, op0=ALU.mult)
 
+        nc.scalar.copy(out=ident16[:], in_=ident[:])
         vbf = {}
         vq = {}
         vq_s = {}
@@ -137,42 +140,48 @@ def tile_controlvariateexp2linearbanditpolicy_d1p_kernel(
         uq_s = {}
         e_t = {}
 
-        def widen(i, on_v):
+        def widen(i, on_v, blocks):
             if i not in vbf:
                 vbf[i] = keep.tile([P, D], BF16, name="vbf", bufs=8, align_bytes=64)
-            nv = WV[i]
-            for j in range(0 if on_v else nv, nv if on_v else 8):
+            for j in blocks:
                 src = v_u8[i][:, P * j : P * (j + 1)].bitcast(FP8)
                 dst = vbf[i][:, P * j : P * (j + 1)]
                 col = vs[:, i, j : j + 1]
-                if j < nv:
+                if on_v:
                     nc.vector.tensor_scalar(out=dst, in0=src, scalar1=col, scalar2=None, op0=ALU.mult)
                 else:
                     nc.scalar.activation(out=dst, in_=src, func=ACT.Copy, scale=col)
 
         tv = {}
 
-        def turn_v(i):
-            tv[i] = psum.tile([P, 2, 2, P], F32, name="tv", bufs=2)
+        def turn_v(i, passes):
             words = vbf[i][:].bitcast(F32)
-            for gg in range(2):
+            bank = psum.tile([P, len(passes), 2, P], F32, name="tv", bufs=2)
+            for x, gg in enumerate(passes):
                 for u in range(2):
-                    nc.tensor.transpose(tv[i][:, gg, u, :], words[:, 256 * gg + u : 256 * (gg + 1) : 2], ident[:])
+                    nc.tensor.transpose(bank[:, x, u, :], words[:, 256 * gg + u : 256 * (gg + 1) : 2], ident[:])
+            tv[i, passes[0]] = bank
 
-        def take_v(i):
-            v4[i] = keep.tile([P, 2, P, 4], BF16, name="v4", bufs=8, align_bytes=64)
+        def take_v(i, passes):
+            if i not in v4:
+                v4[i] = keep.tile([P, 2, P, 4], BF16, name="v4", bufs=8, align_bytes=64)
             nc.scalar.copy(
-                out=v4[i][:].rearrange("p g r t -> p (g r t)").bitcast(F32).rearrange("p (g r u) -> p g r u", g=2, u=2),
-                in_=tv[i][:].rearrange("p g u r -> p g r u"),
+                out=v4[i][:, passes[0] : passes[-1] + 1]
+                .rearrange("p g r t -> p (g r t)")
+                .bitcast(F32)
+                .rearrange("p (g r u) -> p g r u", r=P, u=2),
+                in_=tv[i, passes[0]][:].rearrange("p g u r -> p g r u"),
             )
 
-        def quant(src, i, codes, scales, name, nb):
-            codes[i] = keep.tile([P, 2, P], U32, name=name + "_codes", bufs=nb, align_bytes=64)
-            scales[i] = keep.tile([P, 2, P], U8, name=name + "_sc", bufs=nb, align_bytes=64)
+        def quant(src, i, codes, scales, name, nb, passes):
+            if i not in codes:
+                codes[i] = keep.tile([P, 2, P], U32, name=name + "_codes", bufs=nb, align_bytes=64)
+                scales[i] = keep.tile([P, 2, P], U8, name=name + "_sc", bufs=nb, align_bytes=64)
+            part = slice(passes[0], passes[-1] + 1)
             nc.vector.quantize_mx(
-                out=codes[i][:].rearrange("p g r -> p (g r)").bitcast(E4M3X4),
-                scales=scales[i][:].rearrange("p g r -> p (g r)"),
-                in_=src[i][:].rearrange("p g r t -> p (g r t)"),
+                out=codes[i][:, part].rearrange("p g r -> p (g r)").bitcast(E4M3X4),
+                scales=scales[i][:, part].rearrange("p g r -> p (g r)"),
+                in_=src[i][:, part].rearrange("p g r t -> p (g r t)"),
             )
 
         def mm(i, h, codes, scales, words, wscales, name, into):
@@ -245,13 +254,18 @@ def tile_controlvariateexp2linearbanditpolicy_d1p_kernel(
                 op1=ALU.subtract,
             )
 
-        def expo(i):
-            e_t[i] = keep.tile([P, N], F32, name="e_%d" % i)
+        sum_b = keep.tile([P, 1], F32, name="sum_b")
+
+        def expo(i, cols, acc):
+            if i not in e_t:
+                e_t[i] = keep.tile([P, N], F32, name="e_%d" % i)
             nc.scalar.activation(
-                out=e_t[i][:], in_=y[i][:], func=ACT.Exp, scale=-1.0, bias=y[i][:, 0:1], accum_out=sums[:, i : i + 1]
+                out=e_t[i][:, cols], in_=y[i][:, cols], func=ACT.Exp, scale=-1.0, bias=y[i][:, 0:1], accum_out=acc
             )
 
         def row_factor(a, b):
+            if b == NT:
+                nc.vector.tensor_tensor(out=sums[:, b - 1 : b], in0=sums[:, b - 1 : b], in1=sum_b[:], op=ALU.add)
             nc.vector.reciprocal(out=rec[:, a:b], in_=sums[:, a:b])
             nc.vector.tensor_scalar(
                 out=cc[:, a:b], in0=rec[:, a:b], scalar1=mu_sum[:, 0:1], scalar2=KEEP / MIX, op0=ALU.mult, op1=ALU.mult
@@ -262,26 +276,30 @@ def tile_controlvariateexp2linearbanditpolicy_d1p_kernel(
                 out=e_t[i][:], in0=e_t[i][:], scalar=cc[:, i : i + 1], in1=mu_bc[:], op0=ALU.mult, op1=ALU.add
             )
 
-        def log_store(i):
+        def log_store(i, parts):
             o = keep.tile([P, N], F32, name="o", bufs=4)
-            nc.scalar.activation(out=o[:], in_=e_t[i][:], func=ACT.Ln, scale=kappa[:, 0:1])
-            nc.sync.dma_start(out=out_rows[:, i, :], in_=o[:])
+            w = N // parts
+            for x in range(parts):
+                cols = slice(w * x, w * (x + 1))
+                nc.scalar.activation(out=o[:, cols], in_=e_t[i][:, cols], func=ACT.Ln, scale=kappa[:, 0:1])
+                nc.sync.dma_start(out=out_rows[:, i, cols], in_=o[:, cols])
 
         def run(op):
             k, a = op.split(":")
             a = [int(x) for x in a.split(".")]
             i = a[0]
             h = a[-1]
+            two = (0, 1) if len(a) == 1 else (h,)
             if k == "WV":
-                widen(i, True)
+                widen(i, True, range(WV[i]) if len(a) == 1 else WH[h][0])
             elif k == "WS":
-                widen(i, False)
+                widen(i, False, range(WV[i], 8) if len(a) == 1 else WH[h][1])
             elif k == "Tv":
-                turn_v(i)
+                turn_v(i, two)
             elif k == "E":
-                take_v(i)
+                take_v(i, two)
             elif k == "Qv":
-                quant(v4, i, vq, vq_s, "v", 8)
+                quant(v4, i, vq, vq_s, "v", 8, two)
             elif k == "Mz":
                 mm(i, h, vq, vq_s, pw, ps, "z", z)
             elif k == "L":
@@ -291,13 +309,16 @@ def tile_controlvariateexp2linearbanditpolicy_d1p_kernel(
             elif k == "G":
                 gain(i, h)
             elif k == "Qu":
-                quant(u4, i, uq, uq_s, "u", 3)
+                quant(u4, i, uq, uq_s, "u", 3, (0, 1))
             elif k == "Ms":
                 mm(i, h, uq, uq_s, aw, asc, "s", s)
             elif k == "Y":
                 negy(i, h)
             elif k == "X":
-                expo(i)
+                if len(a) == 1:
+                    expo(i, slice(0, N), sums[:, i : i + 1])
+                else:
+                    expo(i, slice(512 * h, 512 * (h + 1)), sum_b[:] if h else sums[:, i : i + 1])
             elif k == "prep":
                 prep()
             elif k == "mu":
@@ -307,7 +328,7 @@ def tile_controlvariateexp2linearbanditpolicy_d1p_kernel(
             elif k == "R":
                 mix(i)
             elif k == "N":
-                log_store(i)
+                log_store(i, 2 if len(a) > 1 else 1)
 
         for op in ORDER:
             run(op)

@@ -26,7 +26,7 @@ MIX = 0.15
 WV = [5,5,5,3,0,0,0,0]
 LP = [4,5]
 WH = [[(0, 1, 2), (3,)], [(4, 5), (6, 7)]]
-ORDER = "WS:0.0 WV:0.0 Tv:0.0 WS:0.1 WV:0.1 E:0.0 Tv:0.1 E:0.1 WS:1 WV:1 Qv:0.0 Qv:0.1 Tv:1 Mz:0.1 E:1 Mz:0.0 WS:2 WV:2 WS:3 prep:0 L:0.1 Tv:2 L:0.0 Tu:0.1 Qv:1 E:2 Tu:0.0 WV:3 WS:4 G:0.1 Mz:1.1 G:0.0 Mz:1.0 L:1.1 WS:7 Tv:3 L:1.0 Tu:1.1 Qv:2 Tv:4 E:3 Qu:0 G:1.1 Tu:1.0 WS:6 Ms:0.1 Qv:3 G:1.0 Ms:0.0 E:4 Y:0.1 Mz:2.1 WS:5 Y:0.0 Mz:2.0 L:2.1 Tv:6 L:2.0 X:0 Tu:2.1 Qu:1 Tu:2.0 Qv:4 E:6 G:2.1 Ms:1.1 G:2.0 Ms:1.0 Y:1.1 Mz:3.1 Y:1.0 Mz:3.0 Qu:2 Tv:5 X:1 Qv:6 L:3.0 mu:0 Ms:2.0 L:3.1 E:5 Ms:2.1 Y:2.0 Tu:3.1 Y:2.1 Tu:3.0 G:3.1 Mz:4.0 X:2 G:3.0 Tv:7 Qv:5 L:4.0 Qu:3 Mz:4.1 c:0.3 E:7 R:0 Ms:3.0 L:4.1 Ms:3.1 Qv:7 Mz:5.1 Y:3.0 Tu:4.1 Y:3.1 L:5.1 R:2 X:3 Mz:5.0 Tu:4.0 G:4.1 L:5.0 R:1 Tu:5.1 Mz:6.0 G:4.0 N:0 N:1 N:2 G:5.1 Mz:6.1 Qu:4 Tu:5.0 L:6.0 L:6.1 Ms:4.0 G:5.0 Mz:7.1 Y:4.0 Mz:7.0 Qu:5 Ms:4.1 L:7.1 Ms:5.0 L:7.0 Tu:6.0 Y:4.1 Tu:6.1 Y:5.0 Ms:5.1 G:6.0 X:4 G:6.1 Tu:7.0 Y:5.1 Tu:7.1 Qu:6 X:5 G:7.0 Ms:6.0 G:7.1 Ms:6.1 Y:6.0 Qu:7 Y:6.1 Ms:7.0 Ms:7.1 X:6 Y:7.0 Y:7.1 X:7.0 c:3.7 R:3 X:7.1 c:7.8 R:4 R:7 N:3 R:6 N:4 R:5 N:7 N:6 N:5.0".split(" ")
+ORDER = "WS:0.0 WV:0.0 Tv:0.0 WS:0.1 WV:0.1 E:0.0 Tv:0.1 E:0.1 WS:1 WV:1 Qv:0.0 Qv:0.1 WS:2 WS:3 Tv:1 E:1 WV:2 WS:4 Mz:0.0 Mz:0.1 prep:0 mu0:0 L:0.0 L:0.1 Tv:2 Qv:1 E:2 Tu:0.0 Tu:0.1 G:0.0 WV:3 WS:5 Mz:1.0 G:0.1 Mz:1.1 muP:0 L:1.0 mu1:0 L:1.1 mu2:0 Qu:0 Tv:3 Qv:2 E:3 Tu:1.0 Tu:1.1 G:1.0 mu3:0 WS:6 Ms:0.0 Mz:2.0 G:1.1 Mz:2.1 Y:0.0 Ms:0.1 L:2.0 L:2.1 Qu:1 Y:0.1 Tv:4 X:0 Qv:3 E:4 Tu:2.0 Tu:2.1 G:2.0 Ms:1.0 WS:7 Mz:3.0 G:2.1 Mz:3.1 Y:1.0 Ms:1.1 L:3.0 L:3.1 Qu:2 Y:1.1 X:1 Tv:5 Qv:4 Tu:3.0 E:5 Tu:3.1 G:3.0 Ms:2.0 Mz:4.0 G:3.1 Mz:4.1 Y:2.0 Ms:2.1 L:4.0 L:4.1 Qu:3 Y:2.1 X:2 Tv:6 Qv:5 Tu:4.0 Tu:4.1 E:6 G:4.0 cr:0.3 Ms:3.0 Mz:5.0 G:4.1 cm:0.3 Mz:5.1 Y:3.0 Ms:3.1 L:5.0 R:2 L:5.1 Qu:4 R:1 Y:3.1 X:3 Tv:7 Qv:6 R:0 Tu:5.0 Tu:5.1 E:7 G:5.0 Ms:4.0 Mz:6.0 G:5.1 Mz:6.1 Y:4.0 Ms:4.1 N:0 N:1 N:2 L:6.0 L:6.1 Qu:5 Y:4.1 X:4 Qv:7 Tu:6.0 Tu:6.1 G:6.0 Ms:5.0 Mz:7.0 G:6.1 Mz:7.1 Y:5.0 Ms:5.1 L:7.0 L:7.1 Qu:6 Y:5.1 X:5 Tu:7.0 Tu:7.1 G:7.0 Ms:6.0 G:7.1 Y:6.0 Ms:6.1 Qu:7 Y:6.1 X:6 Ms:7.0 cr:3.6 Y:7.0 X:7.0 cm:3.6 Ms:7.1 Y:7.1 X:7.1 R:3 R:4 ca:7 R:5 cr:6.8 cm:6.8 R:6 R:7 N:3 N:4 N:5 N:6 N:7.0".split(" ")
 
 
 def tile_controlvariateexp2linearbanditpolicy_d1p_kernel(
@@ -121,13 +121,20 @@ def tile_controlvariateexp2linearbanditpolicy_d1p_kernel(
         def prep():
             nc.vector.tensor_copy(out=sp[:], in_=sp16[:])
 
-        def prep_mu():
-            nc.vector.tensor_reduce(out=mu_part[:], in_=mu_col[:], axis=mybir.AxisListType.X, op=ALU.add)
-            mu_tot = psum.tile([P, 1], F32, name="ut0")
-            nc.tensor.matmul(mu_tot[:], lhsT=ones[:], rhs=mu_part[:], start=True, stop=True)
-            nc.vector.tensor_copy(out=mu_sum[:], in_=mu_tot[:])
-            nc.vector.reciprocal(out=mu_rec[:], in_=mu_sum[:])
-            nc.vector.tensor_scalar(out=kappa[:], in0=mu_rec[:], scalar1=MIX * N, scalar2=None, op0=ALU.mult)
+        mu_tot = []
+
+        def prep_mu(k):
+            if k == "mu0":
+                nc.vector.tensor_reduce(out=mu_part[:], in_=mu_col[:], axis=mybir.AxisListType.X, op=ALU.add)
+            elif k == "muP":
+                mu_tot.append(psum.tile([P, 1], F32, name="ut0"))
+                nc.tensor.matmul(mu_tot[0][:], lhsT=ones[:], rhs=mu_part[:], start=True, stop=True)
+            elif k == "mu1":
+                nc.vector.tensor_copy(out=mu_sum[:], in_=mu_tot[0][:])
+            elif k == "mu2":
+                nc.vector.reciprocal(out=mu_rec[:], in_=mu_sum[:])
+            elif k == "mu3":
+                nc.vector.tensor_scalar(out=kappa[:], in0=mu_rec[:], scalar1=MIX * N, scalar2=None, op0=ALU.mult)
 
         nc.scalar.copy(out=ident16[:], in_=ident[:])
         vbf = {}
@@ -263,10 +270,13 @@ def tile_controlvariateexp2linearbanditpolicy_d1p_kernel(
                 out=e_t[i][:, cols], in_=y[i][:, cols], func=ACT.Exp, scale=-1.0, bias=y[i][:, 0:1], accum_out=acc
             )
 
-        def row_factor(a, b):
-            if b == NT:
-                nc.vector.tensor_tensor(out=sums[:, b - 1 : b], in0=sums[:, b - 1 : b], in1=sum_b[:], op=ALU.add)
+        def row_sum():
+            nc.vector.tensor_tensor(out=sums[:, 7:8], in0=sums[:, 7:8], in1=sum_b[:], op=ALU.add)
+
+        def row_rec(a, b):
             nc.vector.reciprocal(out=rec[:, a:b], in_=sums[:, a:b])
+
+        def row_factor(a, b):
             nc.vector.tensor_scalar(
                 out=cc[:, a:b], in0=rec[:, a:b], scalar1=mu_sum[:, 0:1], scalar2=KEEP / MIX, op0=ALU.mult, op1=ALU.mult
             )
@@ -321,9 +331,13 @@ def tile_controlvariateexp2linearbanditpolicy_d1p_kernel(
                     expo(i, slice(512 * h, 512 * (h + 1)), sum_b[:] if h else sums[:, i : i + 1])
             elif k == "prep":
                 prep()
-            elif k == "mu":
-                prep_mu()
-            elif k == "c":
+            elif k in ("mu0", "muP", "mu1", "mu2", "mu3"):
+                prep_mu(k)
+            elif k == "ca":
+                row_sum()
+            elif k == "cr":
+                row_rec(i, h)
+            elif k == "cm":
                 row_factor(i, h)
             elif k == "R":
                 mix(i)

@@ -23,10 +23,10 @@ ETA = 0.8
 KEEP = 0.85
 MIX = 0.15
 
-WV = [5,5,5,3,0,0,0,0]
+WV = [5,5,4,2,0,0,0,0]
 LP = [4,5]
 WH = [[(0, 1, 2), (3,)], [(4, 5), (6, 7)]]
-ORDER = "WS:0.0 WV:0.0 Tv:0.0 WS:0.1 WV:0.1 E:0.0 Tv:0.1 E:0.1 WS:1 WV:1 Qv:0.0 Qv:0.1 WS:2 WS:3 Tv:1 E:1 WV:2 WS:4 Mz:0.0 Mz:0.1 prep:0 mu0:0 L:0.0 L:0.1 Tv:2 Qv:1 E:2 Tu:0.0 Tu:0.1 G:0.0 WV:3 WS:5 Mz:1.0 G:0.1 Mz:1.1 muP:0 L:1.0 mu1:0 L:1.1 mu2:0 Qu:0 Tv:3 Qv:2 E:3 Tu:1.0 Tu:1.1 G:1.0 mu3:0 WS:6 Ms:0.0 Mz:2.0 G:1.1 Mz:2.1 Y:0.0 Ms:0.1 L:2.0 L:2.1 Qu:1 Y:0.1 Tv:4 X:0 Qv:3 E:4 Tu:2.0 Tu:2.1 G:2.0 Ms:1.0 WS:7 Mz:3.0 G:2.1 Mz:3.1 Y:1.0 Ms:1.1 L:3.0 L:3.1 Qu:2 Y:1.1 X:1 Tv:5 Qv:4 Tu:3.0 E:5 Tu:3.1 G:3.0 Ms:2.0 Mz:4.0 G:3.1 Mz:4.1 Y:2.0 Ms:2.1 L:4.0 L:4.1 Qu:3 Y:2.1 X:2 Tv:6 Qv:5 Tu:4.0 Tu:4.1 E:6 G:4.0 cr:0.3 Ms:3.0 Mz:5.0 G:4.1 cm:0.3 Mz:5.1 Y:3.0 Ms:3.1 L:5.0 R:2 L:5.1 Qu:4 R:1 Y:3.1 X:3 Tv:7 Qv:6 R:0 Tu:5.0 Tu:5.1 E:7 G:5.0 Ms:4.0 Mz:6.0 G:5.1 Mz:6.1 Y:4.0 Ms:4.1 N:0 N:1 N:2 L:6.0 L:6.1 Qu:5 Y:4.1 X:4 Qv:7 Tu:6.0 Tu:6.1 G:6.0 Ms:5.0 Mz:7.0 G:6.1 Mz:7.1 Y:5.0 Ms:5.1 L:7.0 L:7.1 Qu:6 Y:5.1 X:5 Tu:7.0 Tu:7.1 G:7.0 Ms:6.0 G:7.1 Y:6.0 Ms:6.1 Qu:7 Y:6.1 X:6 Ms:7.0 cr:3.6 Y:7.0 X:7.0 cm:3.6 Ms:7.1 Y:7.1 X:7.1 R:3 R:4 ca:7 R:5 cr:6.8 cm:6.8 R:6 R:7 N:3 N:4 N:5 N:6 N:7.0".split(" ")
+ORDER = "WS:0.1 WV:0.1 WV:0.0 WS:0.0 Tv:0.1 WS:1 WV:1 Tv:0.0 E:0.1 E:0.0 Qv:0.1 Tv:1 Qv:0.0 prep:0 Mz:0.1 E:1 Mz:0.0 L:0.1 WS:2 L:0.0 Tu:0.1 WS:3 WV:3 Qv:1 Tu:0.0 WV:2 Mz:1.0 G:0.1 WS:5 Tv:2 G:0.0 mu0:0 Mz:1.1 muP:0 L:1.0 E:2 Tv:3 Qu:0 L:1.1 mu1:0 Tu:1.0 WS:7 Qv:2 Ms:0.0 G:1.0 Ms:0.1 E:3 Y:0.0 Mz:2.1 WS:4 Y:0.1 Mz:2.0 L:2.1 Tu:1.1 L:2.0 X:0 Tv:5 G:1.1 mu2:0 Tu:2.0 Qv:3 mu3:0 E:5 Qu:1 Tu:2.1 WS:6 G:2.0 Ms:1.0 G:2.1 Ms:1.1 Y:1.0 Mz:3.1 Y:1.1 Mz:3.0 Qu:2 X:1 Qv:5 Tv:4 L:3.0 Ms:2.1 L:3.1 E:4 Ms:2.0 Y:2.1 Tu:3.0 Y:2.0 Tu:3.1 Qv:4 X:2 G:3.0 Tv:6 G:3.1 Mz:4.0 E:6 cr:0.3 Mz:4.1 Qu:3 L:4.0 cm:0.3 Qv:6 Ms:3.0 R:0 L:4.1 Ms:3.1 Tu:4.1 Y:3.0 Y:3.1 Mz:5.1 G:4.1 X:3 Mz:5.0 R:1 Tu:4.0 L:5.0 R:2 Tv:7 L:5.1 Mz:6.0 E:7 G:4.0 Mz:6.1 N:0 N:1 N:2 L:6.0 Tu:5.1 Qu:4 L:6.1 Ms:4.0 G:5.1 Ms:4.1 Qv:7 Tu:5.0 Y:4.1 Y:4.0 Mz:7.0 G:5.0 Mz:7.1 L:7.0 Tu:6.1 Qu:5 Tu:6.0 L:7.1 G:6.1 Ms:5.0 G:6.0 Ms:5.1 X:4 Y:5.0 Tu:7.1 Y:5.1 Tu:7.0 Qu:6 X:5 G:7.1 Ms:6.0 G:7.0 Ms:6.1 Y:6.0 Qu:7 Y:6.1 Ms:7.0 cr:3.6 Ms:7.1 X:6 cm:3.6 Y:7.0 Y:7.1 X:7.0 R:4 X:7.1 R:3 ca:7 R:5 N:3 cr:6.8 cm:6.8 R:7 N:4 R:6 N:5 N:7 N:6.0".split(" ")
 
 
 def tile_controlvariateexp2linearbanditpolicy_d1p_kernel(
@@ -57,6 +57,8 @@ def tile_controlvariateexp2linearbanditpolicy_d1p_kernel(
         ident = keep.tile([P, P], F32, name="ident")
         make_identity(nc, ident[:])
         ident16 = keep.tile([P, P], BF16, name="ident16")
+        ones = keep.tile([P, P], F32, name="ones")
+        nc.vector.memset(ones[:], 1.0)
 
         vs = keep.tile([P, NT, 8], F32, name="vscale")
         nc.sync.dma_start(out=vs[:], in_=v_scale.rearrange("(p i) j -> p i j", i=NT))
@@ -89,25 +91,23 @@ def tile_controlvariateexp2linearbanditpolicy_d1p_kernel(
         load_rows(m_rows, m_sb, 0, 1, "m")
         load_v(2, 4)
         load_rows(m_rows, m_sb, 1, 2, "m")
+        mu_col = keep.tile([P, 8], BF16, name="mu_col")
+        nc.sync.dma_start(out=mu_col[:], in_=mu.rearrange("(p i) -> p i", i=8))
         load_v(4, 8)
         asc = load_scales(arms_scales, "asc", nc.sync)
         aw = load_words(arms_words, "aw")
         load_rows(lw_rows, lw_sb, 0, 2, "lw")
         load_rows(m_rows, m_sb, 2, 4, "m")
-        load_rows(m_rows, m_sb, 4, 8, "m")
         load_rows(lw_rows, lw_sb, 2, 4, "lw")
-        load_rows(lw_rows, lw_sb, 4, 8, "lw")
         mu_bc = keep.tile([P, N], BF16, name="mu_bc")
         nc.sync.dma_start(out=mu_bc[:], in_=mu.partition_broadcast(P))
+        load_rows(m_rows, m_sb, 4, 8, "m")
+        load_rows(lw_rows, lw_sb, 4, 8, "lw")
 
         sp16 = keep.tile([P, NT], BF16, name="sp16")
         nc.gpsimd.dma_start(out=sp16[:], in_=surp.rearrange("(p i) -> p i", i=NT))
         g16 = keep.tile([P, 2, 4], BF16, name="g16")
         nc.gpsimd.dma_start(out=g16[:], in_=g.rearrange("(h p t) -> p h t", h=2, t=4))
-        mu_col = keep.tile([P, 8], BF16, name="mu_col")
-        nc.gpsimd.dma_start(out=mu_col[:], in_=mu.rearrange("(p i) -> p i", i=8))
-        ones = keep.tile([P, P], F32, name="ones")
-        nc.gpsimd.memset(ones[:], 1.0)
 
         sums = keep.tile([P, NT], F32, name="sums")
         rec = keep.tile([P, NT], F32, name="rec")
@@ -127,7 +127,7 @@ def tile_controlvariateexp2linearbanditpolicy_d1p_kernel(
             if k == "mu0":
                 nc.vector.tensor_reduce(out=mu_part[:], in_=mu_col[:], axis=mybir.AxisListType.X, op=ALU.add)
             elif k == "muP":
-                mu_tot.append(psum.tile([P, 1], F32, name="ut0"))
+                mu_tot.append(psum.tile([P, 1], F32, name="s0"))
                 nc.tensor.matmul(mu_tot[0][:], lhsT=ones[:], rhs=mu_part[:], start=True, stop=True)
             elif k == "mu1":
                 nc.vector.tensor_copy(out=mu_sum[:], in_=mu_tot[0][:])

from contextlib import ExitStack

import concourse.mybir as mybir
from concourse.masks import make_identity

T, D, N = 1024, 1024, 1024
P = 128
NT = T // P
FLOPS = 2 * T * D * D + 2 * T * D * N

F32 = mybir.dt.float32
BF16 = mybir.dt.bfloat16
I32 = mybir.dt.int32
U32 = mybir.dt.uint32
U8 = mybir.dt.uint8
FP8 = mybir.dt.float8_e4m3fn
E4M3X4 = mybir.dt.float8_e4m3fn_x4
E2M1X4 = mybir.dt.float4_e2m1fn_x4
ALU = mybir.AluOpType
ACT = mybir.ActivationFunctionType

ETA = 0.8
KEEP = 0.85
MIX = 0.15

WV = [5,5,4,2,0,0,0,0]
LP = [4,5]
WH = [[(0, 1, 2), (3,)], [(4, 5), (6, 7)]]
ORDER = "WS:0.1 WV:0.1 WV:0.0 WS:0.0 Tv:0.1 WS:1 WV:1 Tv:0.0 E:0.1 E:0.0 Qv:0.1 Tv:1 Qv:0.0 prep:0 Mz:0.1 E:1 Mz:0.0 L:0.1 WS:2 L:0.0 Tu:0.1 WS:3 WV:3 Qv:1 Tu:0.0 WV:2 Mz:1.0 G:0.1 WS:5 Tv:2 G:0.0 mu0:0 Mz:1.1 muP:0 L:1.0 E:2 Tv:3 Qu:0 L:1.1 mu1:0 Tu:1.0 WS:7 Qv:2 Ms:0.0 G:1.0 Ms:0.1 E:3 Y:0.0 Mz:2.1 WS:4 Y:0.1 Mz:2.0 L:2.1 Tu:1.1 L:2.0 X:0 Tv:5 G:1.1 mu2:0 Tu:2.0 Qv:3 mu3:0 E:5 Qu:1 Tu:2.1 WS:6 G:2.0 Ms:1.0 G:2.1 Ms:1.1 Y:1.0 Mz:3.1 Y:1.1 Mz:3.0 Qu:2 X:1 Qv:5 Tv:4 L:3.0 Ms:2.1 L:3.1 E:4 Ms:2.0 Y:2.1 Tu:3.0 Y:2.0 Tu:3.1 Qv:4 X:2 G:3.0 Tv:6 G:3.1 Mz:4.0 E:6 cr:0.3 Mz:4.1 Qu:3 L:4.0 cm:0.3 Qv:6 Ms:3.0 R:0 L:4.1 Ms:3.1 Tu:4.1 Y:3.0 Y:3.1 Mz:5.1 G:4.1 X:3 Mz:5.0 R:1 Tu:4.0 L:5.0 R:2 Tv:7 L:5.1 Mz:6.0 E:7 G:4.0 Mz:6.1 N:0 N:1 N:2 L:6.0 Tu:5.1 Qu:4 L:6.1 Ms:4.0 G:5.1 Ms:4.1 Qv:7 Tu:5.0 Y:4.1 Y:4.0 Mz:7.0 G:5.0 Mz:7.1 L:7.0 Tu:6.1 Qu:5 Tu:6.0 L:7.1 G:6.1 Ms:5.0 G:6.0 Ms:5.1 X:4 Y:5.0 Tu:7.1 Y:5.1 Tu:7.0 Qu:6 X:5 G:7.1 Ms:6.0 G:7.0 Ms:6.1 Y:6.0 Qu:7 Y:6.1 Ms:7.0 cr:3.6 Ms:7.1 X:6 cm:3.6 Y:7.0 Y:7.1 X:7.0 R:4 X:7.1 R:3 ca:7 R:5 N:3 cr:6.8 cm:6.8 R:7 N:4 R:6 N:5 N:7 N:6.0".split(" ")


def tile_controlvariateexp2linearbanditpolicy_d1p_kernel(
    tc, v_bytes, v_scale, pinv_words, pinv_scales, surp, m, g, arms_words, arms_scales, logw, mu, out
):
    nc = tc.nc
    with ExitStack() as ctx:
        keep = ctx.enter_context(tc.tile_pool(name="keep", bufs=1))
        psum = ctx.enter_context(tc.psum_pool(name="psum", bufs=1))
        ctx.enter_context(tc.manual_schedule())

        def load_scales(hbm, name, eng):
            t = keep.tile([P, 2, N], U8, name=name, align_bytes=64)
            nc.vector.memset(t[:].bitcast(I32), 0)
            view = hbm.bitcast(I32)
            for q in range(4):
                eng.dma_start(
                    out=t[:].bitcast(I32)[32 * q : 32 * q + 4, :, :],
                    in_=view[:, 4 * q : 4 * q + 4, :].rearrange("g q n -> q g n"),
                )
            return t

        def load_words(hbm, name):
            t = keep.tile([P, 2, 2 * N], U8, name=name, align_bytes=64)
            nc.sync.dma_start(out=t[:].bitcast(I32), in_=hbm.bitcast(I32).rearrange("g p c -> p g c"))
            return t

        ident = keep.tile([P, P], F32, name="ident")
        make_identity(nc, ident[:])
        ident16 = keep.tile([P, P], BF16, name="ident16")
        ones = keep.tile([P, P], F32, name="ones")
        nc.vector.memset(ones[:], 1.0)

        vs = keep.tile([P, NT, 8], F32, name="vscale")
        nc.sync.dma_start(out=vs[:], in_=v_scale.rearrange("(p i) j -> p i j", i=NT))
        v_rows = v_bytes.rearrange("(p i) k -> p i k", i=NT)
        m_rows = m.rearrange("(p i) d -> p i d", i=NT)
        lw_rows = logw.rearrange("(p i) n -> p i n", i=NT)
        out_rows = out.rearrange("(p i) n -> p i n", i=NT)

        v_u8 = {}

        def load_v(a, b):
            t = keep.tile([P, b - a, D], U8, name="v_u8_%d" % a, align_bytes=64)
            nc.sync.dma_start(out=t[:], in_=v_rows[:, a:b, :])
            for i in range(a, b):
                v_u8[i] = t[:, i - a, :]

        m_sb = {}
        lw_sb = {}

        def load_rows(rows, into, a, b, name):
            t = keep.tile([P, b - a, 1024], BF16, name="%s_%d" % (name, a), align_bytes=64)
            nc.sync.dma_start(out=t[:], in_=rows[:, a:b, :])
            for i in range(a, b):
                into[i] = t[:, i - a, :]

        load_v(0, 1)
        load_v(1, 2)
        ps = load_scales(pinv_scales, "ps", nc.sync)
        pw = load_words(pinv_words, "pw")
        load_rows(m_rows, m_sb, 0, 1, "m")
        load_v(2, 4)
        load_rows(m_rows, m_sb, 1, 2, "m")
        mu_col = keep.tile([P, 8], BF16, name="mu_col")
        nc.sync.dma_start(out=mu_col[:], in_=mu.rearrange("(p i) -> p i", i=8))
        load_v(4, 8)
        asc = load_scales(arms_scales, "asc", nc.sync)
        aw = load_words(arms_words, "aw")
        load_rows(lw_rows, lw_sb, 0, 2, "lw")
        load_rows(m_rows, m_sb, 2, 4, "m")
        load_rows(lw_rows, lw_sb, 2, 4, "lw")
        mu_bc = keep.tile([P, N], BF16, name="mu_bc")
        nc.sync.dma_start(out=mu_bc[:], in_=mu.partition_broadcast(P))
        load_rows(m_rows, m_sb, 4, 8, "m")
        load_rows(lw_rows, lw_sb, 4, 8, "lw")

        sp16 = keep.tile([P, NT], BF16, name="sp16")
        nc.gpsimd.dma_start(out=sp16[:], in_=surp.rearrange("(p i) -> p i", i=NT))
        g16 = keep.tile([P, 2, 4], BF16, name="g16")
        nc.gpsimd.dma_start(out=g16[:], in_=g.rearrange("(h p t) -> p h t", h=2, t=4))

        sums = keep.tile([P, NT], F32, name="sums")
        rec = keep.tile([P, NT], F32, name="rec")
        cc = keep.tile([P, NT], F32, name="cc")
        sp = keep.tile([P, NT], F32, name="sp")
        mu_part = keep.tile([P, 1], F32, name="mu_part")
        mu_sum = keep.tile([P, 1], F32, name="mu_sum")
        mu_rec = keep.tile([P, 1], F32, name="mu_rec")
        kappa = keep.tile([P, 1], F32, name="kappa")

        def prep():
            nc.vector.tensor_copy(out=sp[:], in_=sp16[:])

        mu_tot = []

        def prep_mu(k):
            if k == "mu0":
                nc.vector.tensor_reduce(out=mu_part[:], in_=mu_col[:], axis=mybir.AxisListType.X, op=ALU.add)
            elif k == "muP":
                mu_tot.append(psum.tile([P, 1], F32, name="s0"))
                nc.tensor.matmul(mu_tot[0][:], lhsT=ones[:], rhs=mu_part[:], start=True, stop=True)
            elif k == "mu1":
                nc.vector.tensor_copy(out=mu_sum[:], in_=mu_tot[0][:])
            elif k == "mu2":
                nc.vector.reciprocal(out=mu_rec[:], in_=mu_sum[:])
            elif k == "mu3":
                nc.vector.tensor_scalar(out=kappa[:], in0=mu_rec[:], scalar1=MIX * N, scalar2=None, op0=ALU.mult)

        nc.scalar.copy(out=ident16[:], in_=ident[:])
        vbf = {}
        vq = {}
        vq_s = {}
        v4 = {}
        lh = {}
        u4 = {}
        uq = {}
        uq_s = {}
        e_t = {}

        def widen(i, on_v, blocks):
            if i not in vbf:
                vbf[i] = keep.tile([P, D], BF16, name="vbf", bufs=8, align_bytes=64)
            for j in blocks:
                src = v_u8[i][:, P * j : P * (j + 1)].bitcast(FP8)
                dst = vbf[i][:, P * j : P * (j + 1)]
                col = vs[:, i, j : j + 1]
                if on_v:
                    nc.vector.tensor_scalar(out=dst, in0=src, scalar1=col, scalar2=None, op0=ALU.mult)
                else:
                    nc.scalar.activation(out=dst, in_=src, func=ACT.Copy, scale=col)

        tv = {}

        def turn_v(i, passes):
            words = vbf[i][:].bitcast(F32)
            bank = psum.tile([P, len(passes), 2, P], F32, name="tv", bufs=2)
            for x, gg in enumerate(passes):
                for u in range(2):
                    nc.tensor.transpose(bank[:, x, u, :], words[:, 256 * gg + u : 256 * (gg + 1) : 2], ident[:])
            tv[i, passes[0]] = bank

        def take_v(i, passes):
            if i not in v4:
                v4[i] = keep.tile([P, 2, P, 4], BF16, name="v4", bufs=8, align_bytes=64)
            nc.scalar.copy(
                out=v4[i][:, passes[0] : passes[-1] + 1]
                .rearrange("p g r t -> p (g r t)")
                .bitcast(F32)
                .rearrange("p (g r u) -> p g r u", r=P, u=2),
                in_=tv[i, passes[0]][:].rearrange("p g u r -> p g r u"),
            )

        def quant(src, i, codes, scales, name, nb, passes):
            if i not in codes:
                codes[i] = keep.tile([P, 2, P], U32, name=name + "_codes", bufs=nb, align_bytes=64)
                scales[i] = keep.tile([P, 2, P], U8, name=name + "_sc", bufs=nb, align_bytes=64)
            part = slice(passes[0], passes[-1] + 1)
            nc.vector.quantize_mx(
                out=codes[i][:, part].rearrange("p g r -> p (g r)").bitcast(E4M3X4),
                scales=scales[i][:, part].rearrange("p g r -> p (g r)"),
                in_=src[i][:, part].rearrange("p g r t -> p (g r t)"),
            )

        def mm(i, h, codes, scales, words, wscales, name, into):
            bank = psum.tile([P, 512], F32, name="%s%d" % (name, h))
            for gg in range(2):
                nc.tensor.matmul_mx(
                    out=bank[:],
                    lhsT=codes[i][:, gg, :].bitcast(E4M3X4),
                    lhsT_scale=scales[i][:, gg, :],
                    rhs=words[:, gg, 1024 * h : 1024 * (h + 1)].bitcast(E2M1X4),
                    rhs_scale=wscales[:, gg, 512 * h : 512 * (h + 1)],
                    start=(gg == 0),
                    stop=(gg == 1),
                )
            into[i, h] = bank

        z = {}
        s = {}

        def lhat(i, h):
            lh[i, h] = keep.tile([P, 4, P], F32, name="lh%d" % h, bufs=4, align_bytes=64)
            zv = z[i, h][:].rearrange("q (p t) -> q t p", t=4)
            if i in LP:
                nc.scalar.activation(out=lh[i, h][:], in_=zv, func=ACT.Copy, scale=sp[:, i : i + 1])
                return
            nc.vector.scalar_tensor_tensor(
                out=lh[i, h][:],
                in0=zv,
                scalar=sp[:, i : i + 1],
                in1=m_sb[i][:, 512 * h : 512 * (h + 1)].rearrange("q (p t) -> q t p", t=4),
                op0=ALU.mult,
                op1=ALU.add,
            )

        ut = {}

        def turn_u(i, h):
            bank = psum.tile([P, 4, P], F32, name="ut%d" % h)
            for t in range(4):
                if i in LP:
                    nc.tensor.matmul(
                        bank[:, t, :], lhsT=m_sb[i][:, 512 * h + t : 512 * (h + 1) : 4], rhs=ident16[:], start=True, stop=False
                    )
                    nc.tensor.matmul(bank[:, t, :], lhsT=lh[i, h][:, t, :], rhs=ident[:], is_transpose=True, start=False, stop=True)
                else:
                    nc.tensor.transpose(bank[:, t, :], lh[i, h][:, t, :], ident[:])
            ut[i, h] = bank

        def gain(i, h):
            if i not in u4:
                u4[i] = keep.tile([P, 2, P, 4], BF16, name="u4", bufs=3, align_bytes=64)
            nc.vector.tensor_tensor(
                out=u4[i][:, h],
                in0=ut[i, h][:].rearrange("p t r -> p r t"),
                in1=g16[:, h, :].unsqueeze(1).to_broadcast([P, P, 4]),
                op=ALU.mult,
            )

        y = {}

        def negy(i, h):
            if i not in y:
                y[i] = keep.tile([P, N], F32, name="y", bufs=4)
            nc.vector.scalar_tensor_tensor(
                out=y[i][:, 512 * h : 512 * (h + 1)],
                in0=s[i, h][:],
                scalar=ETA,
                in1=lw_sb[i][:, 512 * h : 512 * (h + 1)],
                op0=ALU.mult,
                op1=ALU.subtract,
            )

        sum_b = keep.tile([P, 1], F32, name="sum_b")

        def expo(i, cols, acc):
            if i not in e_t:
                e_t[i] = keep.tile([P, N], F32, name="e_%d" % i)
            nc.scalar.activation(
                out=e_t[i][:, cols], in_=y[i][:, cols], func=ACT.Exp, scale=-1.0, bias=y[i][:, 0:1], accum_out=acc
            )

        def row_sum():
            nc.vector.tensor_tensor(out=sums[:, 7:8], in0=sums[:, 7:8], in1=sum_b[:], op=ALU.add)

        def row_rec(a, b):
            nc.vector.reciprocal(out=rec[:, a:b], in_=sums[:, a:b])

        def row_factor(a, b):
            nc.vector.tensor_scalar(
                out=cc[:, a:b], in0=rec[:, a:b], scalar1=mu_sum[:, 0:1], scalar2=KEEP / MIX, op0=ALU.mult, op1=ALU.mult
            )

        def mix(i):
            nc.vector.scalar_tensor_tensor(
                out=e_t[i][:], in0=e_t[i][:], scalar=cc[:, i : i + 1], in1=mu_bc[:], op0=ALU.mult, op1=ALU.add
            )

        def log_store(i, parts):
            o = keep.tile([P, N], F32, name="o", bufs=4)
            w = N // parts
            for x in range(parts):
                cols = slice(w * x, w * (x + 1))
                nc.scalar.activation(out=o[:, cols], in_=e_t[i][:, cols], func=ACT.Ln, scale=kappa[:, 0:1])
                nc.sync.dma_start(out=out_rows[:, i, cols], in_=o[:, cols])

        def run(op):
            k, a = op.split(":")
            a = [int(x) for x in a.split(".")]
            i = a[0]
            h = a[-1]
            two = (0, 1) if len(a) == 1 else (h,)
            if k == "WV":
                widen(i, True, range(WV[i]) if len(a) == 1 else WH[h][0])
            elif k == "WS":
                widen(i, False, range(WV[i], 8) if len(a) == 1 else WH[h][1])
            elif k == "Tv":
                turn_v(i, two)
            elif k == "E":
                take_v(i, two)
            elif k == "Qv":
                quant(v4, i, vq, vq_s, "v", 8, two)
            elif k == "Mz":
                mm(i, h, vq, vq_s, pw, ps, "z", z)
            elif k == "L":
                lhat(i, h)
            elif k == "Tu":
                turn_u(i, h)
            elif k == "G":
                gain(i, h)
            elif k == "Qu":
                quant(u4, i, uq, uq_s, "u", 3, (0, 1))
            elif k == "Ms":
                mm(i, h, uq, uq_s, aw, asc, "s", s)
            elif k == "Y":
                negy(i, h)
            elif k == "X":
                if len(a) == 1:
                    expo(i, slice(0, N), sums[:, i : i + 1])
                else:
                    expo(i, slice(512 * h, 512 * (h + 1)), sum_b[:] if h else sums[:, i : i + 1])
            elif k == "prep":
                prep()
            elif k in ("mu0", "muP", "mu1", "mu2", "mu3"):
                prep_mu(k)
            elif k == "ca":
                row_sum()
            elif k == "cr":
                row_rec(i, h)
            elif k == "cm":
                row_factor(i, h)
            elif k == "R":
                mix(i)
            elif k == "N":
                log_store(i, 2 if len(a) > 1 else 1)

        for op in ORDER:
            run(op)
